import numpy as np
import ml_dtypes


def mxq(x, axis, fmt="e4m3"):
    dtype, down = {"e4m3": (ml_dtypes.float8_e4m3fn, 7), "e5m2": (ml_dtypes.float8_e5m2, 14)}[fmt]
    v = np.moveaxis(np.asarray(x, np.float32).astype(ml_dtypes.bfloat16).astype(np.float64), axis, -1)
    blocks = v.reshape(v.shape[:-1] + (-1, 32))
    amax = np.abs(blocks).max(-1, keepdims=True)
    byte = np.maximum(np.where(amax > 0, np.frexp(amax)[1] - 1 + 127, 0) - down, 1)
    scale = np.exp2(byte - 127.0)
    codes = (blocks / scale).astype(np.float32).astype(dtype).astype(np.float64)
    return np.moveaxis((codes * scale).reshape(v.shape), -1, axis)


WIDE = False


def mx_kscale(k):
    if not WIDE:
        return np.ones(k)
    levels = np.array([10, -10, 5, -5, 0])
    if k % 512:
        return np.exp2(np.random.permutation(np.resize(levels, k // 32))).repeat(32)
    a = np.empty((k // 512, 16))
    for p in range(k // 512):
        a[p, :8] = np.random.permutation(np.resize(levels, 8))
        for g in range(8):
            far = levels[np.abs(levels - a[p, g]) >= 10]
            a[p, g + 8] = far[np.random.randint(len(far))]
    return np.exp2(a.ravel()).repeat(32)


BF16 = ml_dtypes.bfloat16


def bf(x):
    return np.asarray(x, np.float32).astype(BF16)


def f64(x):
    return np.asarray(x).astype(np.float64)


T, K, J, V, R = 1024, 1024, 512, 2048, 512


def draw0():
    s = mx_kscale(K)
    r = mx_kscale(J)
    t = mx_kscale(T)
    x = np.random.standard_normal((T, K)) * s
    w_full = np.random.standard_normal((K, V)) / np.sqrt(K) / s[:, None]
    d = np.random.standard_normal((T, J)) * r
    w_draft = np.random.standard_normal((J, V)) / np.sqrt(J) / r[:, None]
    accept = np.random.uniform(0.5, 1.5, T) * t
    f = np.random.standard_normal((T, R)) / np.sqrt(T) / t[:, None]
    return {"x": bf(x), "w_full": bf(w_full),
            "d": bf(d), "w_draft": bf(w_draft),
            "accept": bf(accept), "f": bf(f)}


def core(x, w_full, d, w_draft, accept, f):
    full = mxq(f64(x), 1, "e4m3") @ mxq(f64(w_full), 0, "e4m3")
    draft = mxq(f64(d), 1, "e4m3") @ mxq(f64(w_draft), 0, "e4m3")
    e = np.tanh(full - draft) * f64(accept)[:, None]
    return mxq(f64(f), 0, "e4m3").T @ mxq(e, 0, "e4m3")


def e4m3fn_bytes(y):
    return np.clip(np.asarray(y, np.float64), -448.0, 448.0).astype(np.float32).astype(ml_dtypes.float8_e4m3fn).view(np.uint8)


def e4m3fn_values(b):
    return np.asarray(b, np.uint8).view(ml_dtypes.float8_e4m3fn).astype(np.float64)


def setup_inputs():
    d = draw0()
    x0 = np.asarray(d['w_full']).astype(np.float64)
    s = (np.max(np.abs(x0), axis=(1,), keepdims=True) / 448.0).astype(np.float32)
    out = {}
    for k, v in d.items():
        if k == 'w_full':
            out['w_full_bytes'] = e4m3fn_bytes(x0 / s.astype(np.float64))
            out['w_full_scale'] = s
        else:
            out[k] = v
    return out


def reference(x, w_full_bytes, w_full_scale, d, w_draft, accept, f):
    return core(x, e4m3fn_values(w_full_bytes) * w_full_scale.astype(np.float64), d, w_draft, accept, f)

@@ -1,0 +1,276 @@
+from contextlib import ExitStack
+
+import concourse.mybir as mybir
+from concourse.masks import make_identity
+
+T, K, J, V, R = 1024, 1024, 512, 2048, 512
+FLOPS = 2 * T * K * V + 2 * T * J * V + 2 * R * T * V
+
+F32 = mybir.dt.float32
+BF16 = mybir.dt.bfloat16
+U32 = mybir.dt.uint32
+U8 = mybir.dt.uint8
+FP8 = mybir.dt.float8_e4m3fn
+FP8X4 = mybir.dt.float8_e4m3fn_x4
+MULT = mybir.AluOpType.mult
+TANH = mybir.ActivationFunctionType.Tanh
+COPY = mybir.ActivationFunctionType.Copy
+
+P = 128
+NG = 2
+NB = 256
+BLOCKS = V // NB
+SB = 512
+STRETCHES = V // SB
+RT = R // P
+
+
+def tile_draft_logit_correction_s7_kernel(tc, x, w_bytes, w_scale, d, w_draft, accept, f, out):
+    nc = tc.nc
+    with ExitStack() as ctx:
+        keep = ctx.enter_context(tc.tile_pool(name="keep", bufs=1))
+        work = ctx.enter_context(tc.tile_pool(name="work", bufs=4))
+        psum = ctx.enter_context(tc.psum_pool(name="psum", bufs=6))
+        opsum = ctx.enter_context(tc.psum_pool(name="opsum", bufs=2))
+
+        ident = keep.tile([P, P], F32, name="ident")
+        make_identity(nc, ident[:])
+        warm = keep.tile([P, 1], F32, name="warm")
+        nc.vector.memset(warm[:], 0.0)
+        nc.scalar.activation(out=warm[:], in_=warm[:], func=TANH)
+
+        x_v = x.rearrange("(g p t) k -> g p t k", p=P, t=4)
+        d_v = d.rearrange("(g p t) k -> g p t k", p=P, t=4)
+        wb_v = w_bytes.rearrange("(g p t) n -> g p t n", p=P, t=4)
+        wd_v = w_draft.rearrange("(p t) n -> p t n", t=4)
+        f_v = f.rearrange("(g p t) r -> g p t r", p=P, t=4)
+
+        scale = keep.tile([P, NG, 4], F32, name="scale")
+        nc.sync.dma_start(out=scale[:], in_=w_scale.rearrange("(g p t) o -> p g (t o)", p=P, t=4))
+        wbytes = {}
+        wdraw = {}
+        xraw = {}
+        draw = {}
+        fraw = {}
+
+        def load_wb(g, lo, hi):
+            tile = keep.tile([P, 4, hi - lo], U8, name="wbytes_%d_%d" % (g, lo))
+            nc.sync.dma_start(out=tile[:], in_=wb_v[g][:, :, lo:hi])
+            wbytes[g, lo] = tile
+
+        def load_wd(s):
+            wdraw[s] = keep.tile([P, 4, SB], BF16, name="wdraw_%d" % s)
+            nc.sync.dma_start(out=wdraw[s][:], in_=wd_v[:, :, s * SB:(s + 1) * SB])
+
+        def load_x(g, h):
+            xraw[g, h] = keep.tile([P, 2, K], BF16, name="xraw_%d_%d" % (g, h))
+            nc.sync.dma_start(out=xraw[g, h][:], in_=x_v[g][:, 2 * h:2 * h + 2, :])
+
+        def load_d(g):
+            draw[g] = keep.tile([P, 4, J], BF16, name="draw_%d" % g)
+            nc.sync.dma_start(out=draw[g][:], in_=d_v[g])
+
+        def load_f(g):
+            fraw[g] = keep.tile([P, 4, R], BF16, name="fraw_%d" % g)
+            nc.sync.dma_start(out=fraw[g][:], in_=f_v[g])
+
+        load_wb(0, 0, 512)
+        load_x(0, 0)
+        load_wd(0)
+        load_x(0, 1)
+        load_wb(1, 0, 512)
+        load_d(0)
+        acc_raw = keep.tile([P, NG, 4], BF16, name="acc_raw")
+        nc.sync.dma_start(out=acc_raw[:], in_=accept.rearrange("(g p t) -> p g t", p=P, t=4))
+        load_x(1, 0)
+        load_x(1, 1)
+        load_d(1)
+        load_wb(0, 512, 1024)
+        load_wb(1, 512, 1024)
+        load_f(0)
+        load_f(1)
+        load_wd(1)
+        load_wb(0, 1024, 2048)
+        load_wb(1, 1024, 2048)
+        load_wd(2)
+        load_wd(3)
+        acc = keep.tile([P, NG, 4], F32, name="acc")
+
+        x_codes, x_scales, d_codes, d_scales = {}, {}, {}, {}
+
+        def tokens_x(g, t):
+            words = xraw[g, t // 2][:, t % 2, :].bitcast(F32)
+            bank = psum.tile([P, 2, 2, P], F32, name="xt", tag="bank")
+            for kg in range(2):
+                for u in range(2):
+                    nc.tensor.transpose(bank[:, kg, u, :], words[:, 256 * kg + u:256 * (kg + 1):2], ident[:])
+            xi = work.tile([P, 2, P, 4], BF16, name="xi", tag="xi", align_bytes=64)
+            nc.scalar.copy(out=xi[:].bitcast(F32), in_=bank[:].rearrange("p k u r -> p k r u"))
+            codes = keep.tile([P, 2, P], U32, name="xc_%d_%d" % (g, t), align_bytes=64)
+            scales = keep.tile([P, 2, P], U8, name="xs_%d_%d" % (g, t), align_bytes=64)
+            nc.vector.quantize_mx(out=codes[:].rearrange("p k r -> p (k r)").bitcast(FP8X4),
+                                  scales=scales[:].rearrange("p k r -> p (k r)"),
+                                  in_=xi[:].rearrange("p k r j -> p (k r j)"))
+            x_codes[g, t] = codes
+            x_scales[g, t] = scales
+
+        def tokens_d(g, h):
+            bank = psum.tile([P, 2, 2, P], F32, name="dt", tag="bank")
+            for tt in range(2):
+                words = draw[g][:, 2 * h + tt, :].bitcast(F32)
+                for u in range(2):
+                    nc.tensor.transpose(bank[:, tt, u, :], words[:, u::2], ident[:])
+            di = work.tile([P, 2, P, 4], BF16, name="di", tag="xi", align_bytes=64)
+            nc.scalar.copy(out=di[:].bitcast(F32), in_=bank[:].rearrange("p k u r -> p k r u"))
+            codes = keep.tile([P, 2, P], U32, name="dc_%d_%d" % (g, h), align_bytes=64)
+            scales = keep.tile([P, 2, P], U8, name="ds_%d_%d" % (g, h), align_bytes=64)
+            nc.vector.quantize_mx(out=codes[:].rearrange("p k r -> p (k r)").bitcast(FP8X4),
+                                  scales=scales[:].rearrange("p k r -> p (k r)"),
+                                  in_=di[:].rearrange("p k r j -> p (k r j)"))
+            for tt in range(2):
+                d_codes[g, 2 * h + tt] = codes[:, tt, :]
+                d_scales[g, 2 * h + tt] = scales[:, tt, :]
+
+        def quantize(name, src, width):
+            codes = keep.tile([P, width], U32, name=name + "_c", align_bytes=64)
+            scales = keep.tile([P, width], U8, name=name + "_s", align_bytes=64)
+            nc.vector.quantize_mx(out=codes[:].bitcast(FP8X4), scales=scales[:],
+                                  in_=src[:].rearrange("p n j -> p (n j)"))
+            return codes, scales
+
+        def views(dst, src):
+            return (dst[:].rearrange("p (c i) t -> p c t i", i=4), src.rearrange("p t (c i) -> p c t i", i=4))
+
+        w_op, wd_op, f_op = {}, {}, {}
+
+        plains = {}
+
+        def widen(g, lo, hi):
+            plain = work.tile([P, 4, hi - lo], BF16, name="wplain", tag="wplain", bufs=4)
+            for t in range(4):
+                nc.vector.tensor_scalar(out=plain[:, t, :], in0=wbytes[g, lo][:, t, :].bitcast(FP8),
+                                        scalar1=scale[:, g, t:t + 1], scalar2=None, op0=MULT)
+            for c in range(lo, hi, SB):
+                plains[g, c // SB] = plain[:, :, c - lo:c - lo + SB]
+
+        def weights(g, s, on_scalar):
+            if s < 3:
+                widen(g, s * SB, (s + 1) * SB if s < 2 else V)
+            plain = plains[g, s]
+            wi = work.tile([P, SB, 4], BF16, name="wi", tag="wi", align_bytes=64)
+            o, i = views(wi, plain)
+            if on_scalar:
+                nc.scalar.copy(out=o, in_=i)
+            else:
+                nc.vector.tensor_copy(out=o, in_=i)
+            w_op[g, s] = quantize("w_%d_%d" % (g, s), wi, SB)
+
+        def draft_weights(s, on_scalar):
+            wdi = work.tile([P, SB, 4], BF16, name="wdi", tag="wi", align_bytes=64)
+            o, i = views(wdi, wdraw[s][:])
+            if on_scalar:
+                nc.scalar.activation(out=o, in_=i, func=COPY, scale=-1.0)
+            else:
+                nc.vector.tensor_scalar(out=o, in0=i, scalar1=-1.0, scalar2=None, op0=MULT)
+            wd_op[s] = quantize("wd_%d" % s, wdi, SB)
+
+        def features(g):
+            fi = work.tile([P, R, 4], BF16, name="fi", tag="wi", align_bytes=64)
+            o, i = views(fi, fraw[g][:])
+            nc.vector.tensor_copy(out=o, in_=i)
+            f_op[g] = quantize("f_%d" % g, fi, R)
+
+        e_op = {}
+
+        def logits(b, g):
+            s, lo = b // 2, (b % 2) * NB
+            cols = slice(lo, lo + NB)
+            th = work.tile([P, 2, NB, 2], F32, name="th", tag="th", bufs=4)
+            for h in range(2):
+                bank = psum.tile([P, 2, NB], F32, name="lg", tag="bank")
+                for jj in range(2):
+                    t = 2 * h + jj
+                    for k in range(3):
+                        if k < 2:
+                            lc, ls = x_codes[g, t][:, k, :], x_scales[g, t][:, k, :]
+                            rc, rs = w_op[k, s]
+                        else:
+                            lc, ls = d_codes[g, t], d_scales[g, t]
+                            rc, rs = wd_op[s]
+                        nc.tensor.matmul_mx(out=bank[:, jj, :], lhsT=lc.bitcast(FP8X4), lhsT_scale=ls,
+                                            rhs=rc[:, cols].bitcast(FP8X4), rhs_scale=rs[:, cols],
+                                            start=(k == 0), stop=(k == 2))
+                nc.scalar.activation(out=th[:, h, :, :], in_=bank[:].rearrange("p j n -> p n j"), func=TANH)
+            return th
+
+        def slope(b, g, th):
+            e = work.tile([P, NB, 4], BF16, name="e", tag="e", align_bytes=64)
+            a = acc[:, g, :].rearrange("p (h j) -> p h j", j=2).unsqueeze(1).to_broadcast([P, NB, 2, 2])
+            nc.vector.tensor_tensor(out=e[:].rearrange("p n (h j) -> p n h j", j=2),
+                                    in0=th[:].rearrange("p h n j -> p n h j"), in1=a, op=MULT)
+            return e
+
+        def slope_q(b, g, e):
+            codes = work.tile([P, NB], U32, name="ec", tag="ec", bufs=6, align_bytes=64)
+            scales = work.tile([P, NB], U8, name="es", tag="es", bufs=6, align_bytes=64)
+            nc.vector.quantize_mx(out=codes[:].bitcast(FP8X4), scales=scales[:],
+                                  in_=e[:].rearrange("p n j -> p (n j)"))
+            e_op[b, g] = codes, scales
+
+        def correction(b):
+            res = work.tile([P, RT, NB], F32, name="res", tag="res")
+            for q in range(2):
+                bank = opsum.tile([P, 2, NB], F32, name="ob", tag="ob")
+                for jj in range(2):
+                    r = 2 * q + jj
+                    for g in range(NG):
+                        fc, fs = f_op[g]
+                        ec, es = e_op[b, g]
+                        nc.tensor.matmul_mx(out=bank[:, jj, :], lhsT=fc[:, r * P:(r + 1) * P].bitcast(FP8X4),
+                                            lhsT_scale=fs[:, r * P:(r + 1) * P],
+                                            rhs=ec[:].bitcast(FP8X4), rhs_scale=es[:],
+                                            start=(g == 0), stop=(g == 1))
+                if b == BLOCKS - 1 and q == 0:
+                    nc.vector.tensor_copy(out=res[:, 0:2, :], in_=bank[:])
+                else:
+                    nc.scalar.copy(out=res[:, 2 * q:2 * q + 2, :], in_=bank[:])
+                nc.sync.dma_start(out=out.rearrange("(r p) v -> p r v", p=P)[:, 2 * q:2 * q + 2, b * NB:(b + 1) * NB],
+                                  in_=res[:, 2 * q:2 * q + 2, :])
+
+        weights(0, 0, False)
+        for t in range(4):
+            tokens_x(0, t)
+        draft_weights(0, True)
+        weights(1, 0, False)
+        tokens_d(0, 0)
+        tokens_d(0, 1)
+        nc.vector.tensor_copy(out=acc[:], in_=acc_raw[:])
+        units = [(b, g) for b in range(BLOCKS) for g in range(NG)]
+        ths, es = {}, {}
+        n = len(units)
+        for i in range(n + 3):
+            if i < n:
+                b, g = units[i]
+                if i == 1:
+                    for t in range(4):
+                        tokens_x(1, t)
+                    tokens_d(1, 0)
+                    tokens_d(1, 1)
+                ths[i] = logits(b, g)
+            if 0 <= i - 1 < n:
+                es[i - 1] = slope(*units[i - 1], ths[i - 1])
+            if 0 <= i - 2 < n:
+                slope_q(*units[i - 2], es[i - 2])
+            if 0 <= i - 3 < n and units[i - 3][1] == 1:
+                correction(units[i - 3][0])
+            if i == 1:
+                features(0)
+                features(1)
+            s = i // 4 + 1
+            if s < STRETCHES:
+                if i % 4 == 0:
+                    weights(0, s, False)
+                if i % 4 == 1:
+                    weights(1, s, True)
+                if i % 4 == 2:
+                    draft_weights(s, True)

@@ -13,6 +13,7 @@ U8 = mybir.dt.uint8
 FP8 = mybir.dt.float8_e4m3fn
 FP8X4 = mybir.dt.float8_e4m3fn_x4
 MULT = mybir.AluOpType.mult
+ADD = mybir.AluOpType.add
 TANH = mybir.ActivationFunctionType.Tanh
 COPY = mybir.ActivationFunctionType.Copy
 
@@ -21,17 +22,74 @@ NG = 2
 NB = 256
 BLOCKS = V // NB
 SB = 512
-STRETCHES = V // SB
 RT = R // P
+UNITS = [(b, g) for b in range(BLOCKS) for g in range(NG)]
+MIX_ON_SCALAR = [[0] * 8, [0] + [1] * 7]
+DMIX = "SSSSSSSS"
+WEIGHT = {"wide": 4, "mix": 2, "fmix": 4, "dmix": 2}
+HEAD, QUOTA, LAG_H, LAG_Q, LAG_C = 38, 5.5, 3, 1, 6
 
 
 def tile_draft_logit_correction_s7_kernel(tc, x, w_bytes, w_scale, d, w_draft, accept, f, out):
     nc = tc.nc
     with ExitStack() as ctx:
         keep = ctx.enter_context(tc.tile_pool(name="keep", bufs=1))
-        work = ctx.enter_context(tc.tile_pool(name="work", bufs=4))
+        work = ctx.enter_context(tc.tile_pool(name="work", bufs=3))
         psum = ctx.enter_context(tc.psum_pool(name="psum", bufs=6))
         opsum = ctx.enter_context(tc.psum_pool(name="opsum", bufs=2))
+
+        ctx.enter_context(tc.manual_schedule())
+
+        x_v = x.rearrange("(g p t) k -> g p t k", p=P, t=4)
+        d_v = d.rearrange("(g p t) k -> g p t k", p=P, t=4)
+        wb_v = w_bytes.rearrange("(g p t) n -> g p t n", p=P, t=4)
+        wd_v = w_draft.rearrange("(p t) n -> p t n", t=4)
+        f_v = f.rearrange("(g p t) r -> g p t r", p=P, t=4)
+        out_v = out.rearrange("(r p) v -> p r v", p=P)
+
+        raw = {}
+
+        def load(key, shape, dtype, src):
+            tile = keep.tile(shape, dtype, name="raw_" + "_".join(str(k) for k in key))
+            nc.sync.dma_start(out=tile[:], in_=src)
+            raw[key] = tile
+
+        def load_wb(g, s, lo, hi):
+            load(("wb", g, s), [P, 4, hi - lo], U8, wb_v[g][:, :, lo:hi])
+
+        def load_wd(s):
+            load(("wd", s), [P, 4, SB], BF16, wd_v[:, :, s * SB:(s + 1) * SB])
+
+        def load_x(g, h):
+            load(("x", g, h), [P, 2, K], BF16, x_v[g][:, 2 * h:2 * h + 2, :])
+
+        def load_d(g):
+            load(("d", g), [P, 4, J], BF16, d_v[g])
+
+        def load_f(g):
+            load(("f", g), [P, 4, R], BF16, f_v[g])
+
+        load(("scale",), [P, NG, 4], F32, w_scale.rearrange("(g p t) o -> p g (t o)", p=P, t=4))
+        load_wb(0, 0, 0, 512)
+        load_x(0, 0)
+        load_wb(1, 0, 0, 512)
+        load_wd(0)
+        load_x(0, 1)
+        load_d(0)
+        load(("accept",), [P, NG, 4], BF16, accept.rearrange("(g p t) -> p g t", p=P, t=4))
+        load_x(1, 0)
+        load_wb(0, 1, 512, 1024)
+        load_x(1, 1)
+        load_wb(1, 1, 512, 1024)
+        load_d(1)
+        load_wd(1)
+        load_wb(0, 2, 1024, 2048)
+        load_f(0)
+        load_wb(1, 2, 1024, 2048)
+        load_wd(2)
+        load_f(1)
+        load_wd(3)
+        scale = raw["scale",]
 
         ident = keep.tile([P, P], F32, name="ident")
         make_identity(nc, ident[:])
@@ -39,238 +97,221 @@ def tile_draft_logit_correction_s7_kernel(tc, x, w_bytes, w_scale, d, w_draft, a
         nc.vector.memset(warm[:], 0.0)
         nc.scalar.activation(out=warm[:], in_=warm[:], func=TANH)
 
-        x_v = x.rearrange("(g p t) k -> g p t k", p=P, t=4)
-        d_v = d.rearrange("(g p t) k -> g p t k", p=P, t=4)
-        wb_v = w_bytes.rearrange("(g p t) n -> g p t n", p=P, t=4)
-        wd_v = w_draft.rearrange("(p t) n -> p t n", t=4)
-        f_v = f.rearrange("(g p t) r -> g p t r", p=P, t=4)
 
-        scale = keep.tile([P, NG, 4], F32, name="scale")
-        nc.sync.dma_start(out=scale[:], in_=w_scale.rearrange("(g p t) o -> p g (t o)", p=P, t=4))
-        wbytes = {}
-        wdraw = {}
-        xraw = {}
-        draw = {}
-        fraw = {}
+        made = {}
 
-        def load_wb(g, lo, hi):
-            tile = keep.tile([P, 4, hi - lo], U8, name="wbytes_%d_%d" % (g, lo))
-            nc.sync.dma_start(out=tile[:], in_=wb_v[g][:, :, lo:hi])
-            wbytes[g, lo] = tile
+        def need(*key):
+            if key not in made:
+                made[key] = makers[key[0]](*key[1:])
+            return made[key]
 
-        def load_wd(s):
-            wdraw[s] = keep.tile([P, 4, SB], BF16, name="wdraw_%d" % s)
-            nc.sync.dma_start(out=wdraw[s][:], in_=wd_v[:, :, s * SB:(s + 1) * SB])
+        def interleaved(dst, src):
+            return (dst[:].rearrange("p (c i) t -> p c t i", i=4), src.rearrange("p t (c i) -> p c t i", i=4))
 
-        def load_x(g, h):
-            xraw[g, h] = keep.tile([P, 2, K], BF16, name="xraw_%d_%d" % (g, h))
-            nc.sync.dma_start(out=xraw[g, h][:], in_=x_v[g][:, 2 * h:2 * h + 2, :])
-
-        def load_d(g):
-            draw[g] = keep.tile([P, 4, J], BF16, name="draw_%d" % g)
-            nc.sync.dma_start(out=draw[g][:], in_=d_v[g])
-
-        def load_f(g):
-            fraw[g] = keep.tile([P, 4, R], BF16, name="fraw_%d" % g)
-            nc.sync.dma_start(out=fraw[g][:], in_=f_v[g])
-
-        load_wb(0, 0, 512)
-        load_x(0, 0)
-        load_wd(0)
-        load_x(0, 1)
-        load_wb(1, 0, 512)
-        load_d(0)
-        acc_raw = keep.tile([P, NG, 4], BF16, name="acc_raw")
-        nc.sync.dma_start(out=acc_raw[:], in_=accept.rearrange("(g p t) -> p g t", p=P, t=4))
-        load_x(1, 0)
-        load_x(1, 1)
-        load_d(1)
-        load_wb(0, 512, 1024)
-        load_wb(1, 512, 1024)
-        load_f(0)
-        load_f(1)
-        load_wd(1)
-        load_wb(0, 1024, 2048)
-        load_wb(1, 1024, 2048)
-        load_wd(2)
-        load_wd(3)
-        acc = keep.tile([P, NG, 4], F32, name="acc")
-
-        x_codes, x_scales, d_codes, d_scales = {}, {}, {}, {}
-
-        def tokens_x(g, t):
-            words = xraw[g, t // 2][:, t % 2, :].bitcast(F32)
-            bank = psum.tile([P, 2, 2, P], F32, name="xt", tag="bank")
-            for kg in range(2):
-                for u in range(2):
-                    nc.tensor.transpose(bank[:, kg, u, :], words[:, 256 * kg + u:256 * (kg + 1):2], ident[:])
-            xi = work.tile([P, 2, P, 4], BF16, name="xi", tag="xi", align_bytes=64)
-            nc.scalar.copy(out=xi[:].bitcast(F32), in_=bank[:].rearrange("p k u r -> p k r u"))
-            codes = keep.tile([P, 2, P], U32, name="xc_%d_%d" % (g, t), align_bytes=64)
-            scales = keep.tile([P, 2, P], U8, name="xs_%d_%d" % (g, t), align_bytes=64)
-            nc.vector.quantize_mx(out=codes[:].rearrange("p k r -> p (k r)").bitcast(FP8X4),
-                                  scales=scales[:].rearrange("p k r -> p (k r)"),
-                                  in_=xi[:].rearrange("p k r j -> p (k r j)"))
-            x_codes[g, t] = codes
-            x_scales[g, t] = scales
-
-        def tokens_d(g, h):
-            bank = psum.tile([P, 2, 2, P], F32, name="dt", tag="bank")
-            for tt in range(2):
-                words = draw[g][:, 2 * h + tt, :].bitcast(F32)
-                for u in range(2):
-                    nc.tensor.transpose(bank[:, tt, u, :], words[:, u::2], ident[:])
-            di = work.tile([P, 2, P, 4], BF16, name="di", tag="xi", align_bytes=64)
-            nc.scalar.copy(out=di[:].bitcast(F32), in_=bank[:].rearrange("p k u r -> p k r u"))
-            codes = keep.tile([P, 2, P], U32, name="dc_%d_%d" % (g, h), align_bytes=64)
-            scales = keep.tile([P, 2, P], U8, name="ds_%d_%d" % (g, h), align_bytes=64)
-            nc.vector.quantize_mx(out=codes[:].rearrange("p k r -> p (k r)").bitcast(FP8X4),
-                                  scales=scales[:].rearrange("p k r -> p (k r)"),
-                                  in_=di[:].rearrange("p k r j -> p (k r j)"))
-            for tt in range(2):
-                d_codes[g, 2 * h + tt] = codes[:, tt, :]
-                d_scales[g, 2 * h + tt] = scales[:, tt, :]
-
-        def quantize(name, src, width):
+        def quantized(name, src, width):
             codes = keep.tile([P, width], U32, name=name + "_c", align_bytes=64)
             scales = keep.tile([P, width], U8, name=name + "_s", align_bytes=64)
             nc.vector.quantize_mx(out=codes[:].bitcast(FP8X4), scales=scales[:],
                                   in_=src[:].rearrange("p n j -> p (n j)"))
             return codes, scales
 
-        def views(dst, src):
-            return (dst[:].rearrange("p (c i) t -> p c t i", i=4), src.rearrange("p t (c i) -> p c t i", i=4))
+        def turn(g, views):
+            bank = psum.tile([P, 2, 2, P], F32, name="turned", tag="bank")
+            for i, words in enumerate(views):
+                for u in range(2):
+                    nc.tensor.transpose(bank[:, i, u, :], words[:, u::2], ident[:])
+            return bank
 
-        w_op, wd_op, f_op = {}, {}, {}
+        def make_xt(g, t):
+            words = raw["x", g, t // 2][:, t % 2, :].bitcast(F32)
+            return turn(g, [words[:, 0:256], words[:, 256:512]])
 
-        plains = {}
+        def make_dt(g, h):
+            return turn(g, [raw["d", g][:, 2 * h + i, :].bitcast(F32) for i in range(2)])
 
-        def widen(g, lo, hi):
-            plain = work.tile([P, 4, hi - lo], BF16, name="wplain", tag="wplain", bufs=4)
+        def emptied(bank):
+            tok = work.tile([P, 2 * P, 4], BF16, name="tok", tag="tok", bufs=6, align_bytes=64)
+            nc.scalar.copy(out=tok[:].bitcast(F32).rearrange("p (i r) u -> p i r u", i=2),
+                           in_=bank[:].rearrange("p i u r -> p i r u"))
+            return tok
+
+        def make_xc(g, t):
+            return emptied(need("xt", g, t))
+
+        def make_dc(g, h):
+            return emptied(need("dt", g, h))
+
+        def make_x(g, t):
+            return quantized("x_%d_%d" % (g, t), need("xc", g, t), 2 * P)
+
+        def make_d(g, h):
+            return quantized("d_%d_%d" % (g, h), need("dc", g, h), 2 * P)
+
+        def make_wide(g, s):
+            plain = work.tile([P, 4, SB], BF16, name="plain", tag="plain", bufs=5)
+            src = raw["wb", g, s] if s < 2 else raw["wb", g, 2]
+            lo = 0 if s < 3 else SB
             for t in range(4):
-                nc.vector.tensor_scalar(out=plain[:, t, :], in0=wbytes[g, lo][:, t, :].bitcast(FP8),
+                nc.vector.tensor_scalar(out=plain[:, t, :], in0=src[:, t, lo:lo + SB].bitcast(FP8),
                                         scalar1=scale[:, g, t:t + 1], scalar2=None, op0=MULT)
-            for c in range(lo, hi, SB):
-                plains[g, c // SB] = plain[:, :, c - lo:c - lo + SB]
+            return plain
 
-        def weights(g, s, on_scalar):
-            if s < 3:
-                widen(g, s * SB, (s + 1) * SB if s < 2 else V)
-            plain = plains[g, s]
-            wi = work.tile([P, SB, 4], BF16, name="wi", tag="wi", align_bytes=64)
-            o, i = views(wi, plain)
-            if on_scalar:
+        def make_mix(g, c):
+            lo = c % 2 * NB
+            src = need("wide", g, c // 2)[:, :, lo:lo + NB]
+            mixed = work.tile([P, NB, 4], BF16, name="mixed", tag="mixed", bufs=10, align_bytes=64)
+            o, i = interleaved(mixed, src)
+            if MIX_ON_SCALAR[g][c]:
                 nc.scalar.copy(out=o, in_=i)
             else:
                 nc.vector.tensor_copy(out=o, in_=i)
-            w_op[g, s] = quantize("w_%d_%d" % (g, s), wi, SB)
+            return mixed
 
-        def draft_weights(s, on_scalar):
-            wdi = work.tile([P, SB, 4], BF16, name="wdi", tag="wi", align_bytes=64)
-            o, i = views(wdi, wdraw[s][:])
-            if on_scalar:
+        def make_dmix(c):
+            lo = c % 2 * NB
+            src = raw["wd", c // 2][:, :, lo:lo + NB]
+            if DMIX[c] == "G":
+                dmixed = work.tile([P, NB, 4], BF16, name="gmixed", tag="gmixed", bufs=2, align_bytes=64)
+                o, i = interleaved(dmixed, src)
+                for h in range(2):
+                    nc.gpsimd.tensor_scalar(out=o[:, 32 * h:32 * h + 32], in0=i[:, 32 * h:32 * h + 32], scalar1=-1.0, scalar2=0.0, op0=MULT, op1=ADD)
+                return dmixed
+            dmixed = work.tile([P, NB, 4], BF16, name="dmixed", tag="mixed", bufs=10, align_bytes=64)
+            o, i = interleaved(dmixed, src)
+            if DMIX[c] == "S":
                 nc.scalar.activation(out=o, in_=i, func=COPY, scale=-1.0)
             else:
                 nc.vector.tensor_scalar(out=o, in0=i, scalar1=-1.0, scalar2=None, op0=MULT)
-            wd_op[s] = quantize("wd_%d" % s, wdi, SB)
+            return dmixed
 
-        def features(g):
-            fi = work.tile([P, R, 4], BF16, name="fi", tag="wi", align_bytes=64)
-            o, i = views(fi, fraw[g][:])
+        def make_w(g, c):
+            return quantized("w_%d_%d" % (g, c), need("mix", g, c), NB)
+
+        def make_wd(c):
+            return quantized("wd_%d" % c, need("dmix", c), NB)
+
+        def make_fmix(g):
+            fmixed = keep.tile([P, R, 4], BF16, name="fmixed_%d" % g, align_bytes=64)
+            o, i = interleaved(fmixed, raw["f", g][:])
             nc.vector.tensor_copy(out=o, in_=i)
-            f_op[g] = quantize("f_%d" % g, fi, R)
+            return fmixed
 
-        e_op = {}
+        def make_f(g):
+            return quantized("f_%d" % g, need("fmix", g), R)
 
-        def logits(b, g):
-            s, lo = b // 2, (b % 2) * NB
-            cols = slice(lo, lo + NB)
-            th = work.tile([P, 2, NB, 2], F32, name="th", tag="th", bufs=4)
+        def make_acc():
+            acc = keep.tile([P, NG, 4], F32, name="acc")
+            nc.vector.tensor_copy(out=acc[:], in_=raw["accept",][:])
+            return acc
+
+        def make_tanh(b, g):
+            th = work.tile([P, 2, NB, 2], F32, name="th", tag="th", bufs=6)
+            terms = [(lambda t: [v[:, 0:P] for v in need("x", g, t)], need("w", 0, b)),
+                     (lambda t: [v[:, P:2 * P] for v in need("x", g, t)], need("w", 1, b)),
+                     (lambda t: [v[:, t % 2 * P:t % 2 * P + P] for v in need("d", g, t // 2)], need("wd", b))]
+            for t in range(4):
+                need("x", g, t)
+            need("d", g, 0)
+            need("d", g, 1)
             for h in range(2):
-                bank = psum.tile([P, 2, NB], F32, name="lg", tag="bank")
+                bank = psum.tile([P, 2, NB], F32, name="logits", tag="bank")
                 for jj in range(2):
-                    t = 2 * h + jj
-                    for k in range(3):
-                        if k < 2:
-                            lc, ls = x_codes[g, t][:, k, :], x_scales[g, t][:, k, :]
-                            rc, rs = w_op[k, s]
-                        else:
-                            lc, ls = d_codes[g, t], d_scales[g, t]
-                            rc, rs = wd_op[s]
+                    for k, (left, right) in enumerate(terms):
+                        lc, ls = left(2 * h + jj)
                         nc.tensor.matmul_mx(out=bank[:, jj, :], lhsT=lc.bitcast(FP8X4), lhsT_scale=ls,
-                                            rhs=rc[:, cols].bitcast(FP8X4), rhs_scale=rs[:, cols],
+                                            rhs=right[0][:].bitcast(FP8X4), rhs_scale=right[1][:],
                                             start=(k == 0), stop=(k == 2))
                 nc.scalar.activation(out=th[:, h, :, :], in_=bank[:].rearrange("p j n -> p n j"), func=TANH)
             return th
 
-        def slope(b, g, th):
-            e = work.tile([P, NB, 4], BF16, name="e", tag="e", align_bytes=64)
-            a = acc[:, g, :].rearrange("p (h j) -> p h j", j=2).unsqueeze(1).to_broadcast([P, NB, 2, 2])
+        def make_slope(b, g):
+            th = need("tanh", b, g)
+            e = work.tile([P, NB, 4], BF16, name="e", tag="e", bufs=4, align_bytes=64)
+            a = need("acc")[:, g, :].rearrange("p (h j) -> p h j", j=2).unsqueeze(1).to_broadcast([P, NB, 2, 2])
             nc.vector.tensor_tensor(out=e[:].rearrange("p n (h j) -> p n h j", j=2),
                                     in0=th[:].rearrange("p h n j -> p n h j"), in1=a, op=MULT)
             return e
 
-        def slope_q(b, g, e):
-            codes = work.tile([P, NB], U32, name="ec", tag="ec", bufs=6, align_bytes=64)
-            scales = work.tile([P, NB], U8, name="es", tag="es", bufs=6, align_bytes=64)
+        def make_e(b, g):
+            e = need("slope", b, g)
+            codes = work.tile([P, NB], U32, name="ec", tag="ec", bufs=12, align_bytes=64)
+            scales = work.tile([P, NB], U8, name="es", tag="es", bufs=12, align_bytes=64)
             nc.vector.quantize_mx(out=codes[:].bitcast(FP8X4), scales=scales[:],
                                   in_=e[:].rearrange("p n j -> p (n j)"))
-            e_op[b, g] = codes, scales
+            return codes, scales
 
-        def correction(b):
-            res = work.tile([P, RT, NB], F32, name="res", tag="res")
+        def make_out(b):
+            for g in range(NG):
+                need("e", b, g)
+                need("f", g)
             for q in range(2):
-                bank = opsum.tile([P, 2, NB], F32, name="ob", tag="ob")
+                res = work.tile([P, 2, NB], F32, name="res", tag="res", bufs=6)
+                bank = opsum.tile([P, 2, NB], F32, name="sums", tag="sums")
                 for jj in range(2):
                     r = 2 * q + jj
                     for g in range(NG):
-                        fc, fs = f_op[g]
-                        ec, es = e_op[b, g]
+                        fc, fs = need("f", g)
+                        ec, es = need("e", b, g)
                         nc.tensor.matmul_mx(out=bank[:, jj, :], lhsT=fc[:, r * P:(r + 1) * P].bitcast(FP8X4),
                                             lhsT_scale=fs[:, r * P:(r + 1) * P],
                                             rhs=ec[:].bitcast(FP8X4), rhs_scale=es[:],
                                             start=(g == 0), stop=(g == 1))
                 if b == BLOCKS - 1 and q == 0:
-                    nc.vector.tensor_copy(out=res[:, 0:2, :], in_=bank[:])
+                    nc.vector.tensor_copy(out=res[:], in_=bank[:])
                 else:
-                    nc.scalar.copy(out=res[:, 2 * q:2 * q + 2, :], in_=bank[:])
-                nc.sync.dma_start(out=out.rearrange("(r p) v -> p r v", p=P)[:, 2 * q:2 * q + 2, b * NB:(b + 1) * NB],
-                                  in_=res[:, 2 * q:2 * q + 2, :])
+                    nc.scalar.copy(out=res[:], in_=bank[:])
+                nc.sync.dma_start(out=out_v[:, 2 * q:2 * q + 2, b * NB:(b + 1) * NB], in_=res[:])
+            return True
 
-        weights(0, 0, False)
-        for t in range(4):
-            tokens_x(0, t)
-        draft_weights(0, True)
-        weights(1, 0, False)
-        tokens_d(0, 0)
-        tokens_d(0, 1)
-        nc.vector.tensor_copy(out=acc[:], in_=acc_raw[:])
-        units = [(b, g) for b in range(BLOCKS) for g in range(NG)]
-        ths, es = {}, {}
-        n = len(units)
-        for i in range(n + 3):
+        makers = {"xt": make_xt, "dt": make_dt, "xc": make_xc, "dc": make_dc, "x": make_x, "d": make_d,
+                  "wide": make_wide, "mix": make_mix, "dmix": make_dmix, "w": make_w, "wd": make_wd,
+                  "fmix": make_fmix, "f": make_f, "acc": make_acc, "tanh": make_tanh, "slope": make_slope,
+                  "e": make_e, "out": make_out}
+
+        prep = [("wide", 0, 0), ("xc", 0, 0), ("xc", 0, 1), ("dmix", 0), ("mix", 0, 0), ("wide", 1, 0),
+                ("x", 0, 0), ("x", 0, 1), ("mix", 1, 0), ("xc", 0, 2), ("xc", 0, 3), ("w", 0, 0), ("wd", 0),
+                ("dc", 0, 0), ("dc", 0, 1), ("x", 0, 2), ("w", 1, 0), ("x", 0, 3), ("mix", 0, 1), ("d", 0, 0),
+                ("dmix", 1), ("d", 0, 1), ("acc",), ("xc", 1, 0), ("xc", 1, 1), ("wide", 0, 1), ("mix", 1, 1), ("w", 0, 1),
+                ("xc", 1, 2), ("xc", 1, 3), ("x", 1, 0), ("wd", 1), ("x", 1, 1), ("dc", 1, 0), ("dc", 1, 1),
+                ("wide", 1, 1), ("w", 1, 1), ("x", 1, 2), ("d", 1, 0), ("x", 1, 3), ("d", 1, 1)]
+        for c in range(2, BLOCKS):
+            prep.append(("dmix", c))
+            for g in range(NG):
+                if c % 2 == 0:
+                    prep.append(("wide", g, c // 2))
+                prep.append(("mix", g, c))
+            if c > 2:
+                prep += [("wd", c - 1), ("w", 0, c - 1), ("w", 1, c - 1)]
+            if c < 4:
+                prep.append(("fmix", c - 2))
+            if c in (3, 5):
+                prep.append(("f", c // 2 - 1))
+        prep += [("wd", BLOCKS - 1), ("w", 0, BLOCKS - 1), ("w", 1, BLOCKS - 1)]
+
+        progress = [0, 0]
+
+        def prepare(target):
+            while progress[0] < len(prep) and progress[1] < target:
+                key = prep[progress[0]]
+                progress[0] += 1
+                if key not in made:
+                    on_vector = key[0] in ("wide", "fmix", "x", "d", "w", "wd", "f")
+                    if key[0] == "mix":
+                        on_vector = not MIX_ON_SCALAR[key[1]][key[2]]
+                    if on_vector:
+                        progress[1] += WEIGHT.get(key[0], 1)
+                    need(*key)
+
+        n = len(UNITS)
+        prepare(HEAD)
+        for i in range(n + LAG_C + 2):
             if i < n:
-                b, g = units[i]
-                if i == 1:
-                    for t in range(4):
-                        tokens_x(1, t)
-                    tokens_d(1, 0)
-                    tokens_d(1, 1)
-                ths[i] = logits(b, g)
-            if 0 <= i - 1 < n:
-                es[i - 1] = slope(*units[i - 1], ths[i - 1])
-            if 0 <= i - 2 < n:
-                slope_q(*units[i - 2], es[i - 2])
-            if 0 <= i - 3 < n and units[i - 3][1] == 1:
-                correction(units[i - 3][0])
-            if i == 1:
-                features(0)
-                features(1)
-            s = i // 4 + 1
-            if s < STRETCHES:
-                if i % 4 == 0:
-                    weights(0, s, False)
-                if i % 4 == 1:
-                    weights(1, s, True)
-                if i % 4 == 2:
-                    draft_weights(s, True)
+                need("tanh", *UNITS[i])
+            prepare(HEAD + QUOTA * (i + 1))
+            if 0 <= i - LAG_H < n:
+                need("slope", *UNITS[i - LAG_H])
+            if 0 <= i - LAG_H - LAG_Q < n:
+                need("e", *UNITS[i - LAG_H - LAG_Q])
+
+            if 0 <= i - LAG_C < n and UNITS[i - LAG_C][1] == 1:
+                need("out", UNITS[i - LAG_C][0])

@@ -24,10 +24,10 @@ BLOCKS = V // NB
 SB = 512
 RT = R // P
 UNITS = [(b, g) for b in range(BLOCKS) for g in range(NG)]
-MIX_ON_SCALAR = [[0] * 8, [0] + [1] * 7]
-DMIX = "SSSSSSSS"
-WEIGHT = {"wide": 4, "mix": 2, "fmix": 4, "dmix": 2}
-HEAD, QUOTA, LAG_H, LAG_Q, LAG_C = 38, 5.5, 3, 1, 6
+WIDE_ON_VECTOR = [[0, 0, 0, 0], [4, 0, 0, 0]]
+MIX_ON_SCALAR = [[0] * 8, [0] * 5 + [1] * 3]
+DMIX = "VVVVVVVV"
+HEAD, QUOTA, LAG_H, LAG_Q, LAG_C = 53, 3.5, 3, 1, 6
 
 
 def tile_draft_logit_correction_s7_kernel(tc, x, w_bytes, w_scale, d, w_draft, accept, f, out):
@@ -49,9 +49,9 @@ def tile_draft_logit_correction_s7_kernel(tc, x, w_bytes, w_scale, d, w_draft, a
 
         raw = {}
 
-        def load(key, shape, dtype, src):
+        def load(key, shape, dtype, src, queue=nc.sync):
             tile = keep.tile(shape, dtype, name="raw_" + "_".join(str(k) for k in key))
-            nc.sync.dma_start(out=tile[:], in_=src)
+            queue.dma_start(out=tile[:], in_=src)
             raw[key] = tile
 
         def load_wb(g, s, lo, hi):
@@ -69,25 +69,25 @@ def tile_draft_logit_correction_s7_kernel(tc, x, w_bytes, w_scale, d, w_draft, a
         def load_f(g):
             load(("f", g), [P, 4, R], BF16, f_v[g])
 
-        load(("scale",), [P, NG, 4], F32, w_scale.rearrange("(g p t) o -> p g (t o)", p=P, t=4))
+        load(("scale",), [P, NG, 4], F32, w_scale.rearrange("(g p t) o -> p g (t o)", p=P, t=4), nc.scalar)
         load_wb(0, 0, 0, 512)
-        load_x(0, 0)
         load_wb(1, 0, 0, 512)
         load_wd(0)
+        load_x(0, 0)
         load_x(0, 1)
         load_d(0)
-        load(("accept",), [P, NG, 4], BF16, accept.rearrange("(g p t) -> p g t", p=P, t=4))
         load_x(1, 0)
-        load_wb(0, 1, 512, 1024)
         load_x(1, 1)
-        load_wb(1, 1, 512, 1024)
         load_d(1)
+        load_wb(0, 1, 512, 1024)
+        load_wb(1, 1, 512, 1024)
+        load(("accept",), [P, NG, 4], BF16, accept.rearrange("(g p t) -> p g t", p=P, t=4), nc.scalar)
         load_wd(1)
-        load_wb(0, 2, 1024, 2048)
         load_f(0)
+        load_wb(0, 2, 1024, 2048)
         load_wb(1, 2, 1024, 2048)
-        load_wd(2)
         load_f(1)
+        load_wd(2)
         load_wd(3)
         scale = raw["scale",]
 
@@ -147,18 +147,26 @@ def tile_draft_logit_correction_s7_kernel(tc, x, w_bytes, w_scale, d, w_draft, a
         def make_d(g, h):
             return quantized("d_%d_%d" % (g, h), need("dc", g, h), 2 * P)
 
-        def make_wide(g, s):
-            plain = work.tile([P, 4, SB], BF16, name="plain", tag="plain", bufs=5)
-            src = raw["wb", g, s] if s < 2 else raw["wb", g, 2]
+        def make_plain(g, s):
+            return work.tile([P, 4, SB], BF16, name="plain", tag="plain", bufs=5)
+
+        def make_wide(engine, g, s):
+            plain = need("plain", g, s)
+            src = raw["wb", g, min(s, 2)]
             lo = 0 if s < 3 else SB
-            for t in range(4):
-                nc.vector.tensor_scalar(out=plain[:, t, :], in0=src[:, t, lo:lo + SB].bitcast(FP8),
-                                        scalar1=scale[:, g, t:t + 1], scalar2=None, op0=MULT)
+            cut = WIDE_ON_VECTOR[g][s]
+            for t in (range(cut) if engine == "V" else range(cut, 4)):
+                codes = src[:, t, lo:lo + SB].bitcast(FP8)
+                if engine == "V":
+                    nc.vector.tensor_scalar(out=plain[:, t, :], in0=codes, scalar1=scale[:, g, t:t + 1], scalar2=None, op0=MULT)
+                else:
+                    nc.scalar.activation(out=plain[:, t, :], in_=codes, func=COPY, scale=scale[:, g, t:t + 1])
             return plain
 
         def make_mix(g, c):
             lo = c % 2 * NB
-            src = need("wide", g, c // 2)[:, :, lo:lo + NB]
+            need("wide", "V", g, c // 2)
+            src = need("wide", "S", g, c // 2)[:, :, lo:lo + NB]
             mixed = work.tile([P, NB, 4], BF16, name="mixed", tag="mixed", bufs=10, align_bytes=64)
             o, i = interleaved(mixed, src)
             if MIX_ON_SCALAR[g][c]:
@@ -240,7 +248,31 @@ def tile_draft_logit_correction_s7_kernel(tc, x, w_bytes, w_scale, d, w_draft, a
                                   in_=e[:].rearrange("p n j -> p (n j)"))
             return codes, scales
 
+        def make_last(b):
+            banks = []
+            for g in range(NG):
+                fc, fs = need("f", g)
+                ec, es = need("e", b, g)
+                for r in range(RT):
+                    if g == 0:
+                        last = psum.tile([P, NB], F32, name="last", tag="bank")
+                        banks.append(last)
+                    nc.tensor.matmul_mx(out=banks[r][:], lhsT=fc[:, r * P:(r + 1) * P].bitcast(FP8X4),
+                                        lhsT_scale=fs[:, r * P:(r + 1) * P],
+                                        rhs=ec[:].bitcast(FP8X4), rhs_scale=es[:],
+                                        start=(g == 0), stop=(g == 1))
+            for r in range(RT):
+                res = work.tile([P, NB], F32, name="res", tag="res", bufs=6)
+                if r % 2 == 0:
+                    nc.vector.tensor_copy(out=res[:], in_=banks[r][:])
+                else:
+                    nc.scalar.copy(out=res[:], in_=banks[r][:])
+                nc.sync.dma_start(out=out_v[:, r, b * NB:(b + 1) * NB], in_=res[:])
+            return True
+
         def make_out(b):
+            if b == BLOCKS - 1:
+                return make_last(b)
             for g in range(NG):
                 need("e", b, g)
                 need("f", g)
@@ -256,29 +288,27 @@ def tile_draft_logit_correction_s7_kernel(tc, x, w_bytes, w_scale, d, w_draft, a
                                             lhsT_scale=fs[:, r * P:(r + 1) * P],
                                             rhs=ec[:].bitcast(FP8X4), rhs_scale=es[:],
                                             start=(g == 0), stop=(g == 1))
-                if b == BLOCKS - 1 and q == 0:
-                    nc.vector.tensor_copy(out=res[:], in_=bank[:])
-                else:
-                    nc.scalar.copy(out=res[:], in_=bank[:])
+                nc.scalar.copy(out=res[:], in_=bank[:])
                 nc.sync.dma_start(out=out_v[:, 2 * q:2 * q + 2, b * NB:(b + 1) * NB], in_=res[:])
             return True
 
         makers = {"xt": make_xt, "dt": make_dt, "xc": make_xc, "dc": make_dc, "x": make_x, "d": make_d,
-                  "wide": make_wide, "mix": make_mix, "dmix": make_dmix, "w": make_w, "wd": make_wd,
+                  "plain": make_plain, "wide": make_wide, "mix": make_mix, "dmix": make_dmix, "w": make_w, "wd": make_wd,
                   "fmix": make_fmix, "f": make_f, "acc": make_acc, "tanh": make_tanh, "slope": make_slope,
                   "e": make_e, "out": make_out}
 
-        prep = [("wide", 0, 0), ("xc", 0, 0), ("xc", 0, 1), ("dmix", 0), ("mix", 0, 0), ("wide", 1, 0),
-                ("x", 0, 0), ("x", 0, 1), ("mix", 1, 0), ("xc", 0, 2), ("xc", 0, 3), ("w", 0, 0), ("wd", 0),
-                ("dc", 0, 0), ("dc", 0, 1), ("x", 0, 2), ("w", 1, 0), ("x", 0, 3), ("mix", 0, 1), ("d", 0, 0),
-                ("dmix", 1), ("d", 0, 1), ("acc",), ("xc", 1, 0), ("xc", 1, 1), ("wide", 0, 1), ("mix", 1, 1), ("w", 0, 1),
-                ("xc", 1, 2), ("xc", 1, 3), ("x", 1, 0), ("wd", 1), ("x", 1, 1), ("dc", 1, 0), ("dc", 1, 1),
-                ("wide", 1, 1), ("w", 1, 1), ("x", 1, 2), ("d", 1, 0), ("x", 1, 3), ("d", 1, 1)]
+        prep = [("wide", "S", 0, 0), ("wide", "V", 1, 0), ("mix", 1, 0), ("mix", 1, 1), ("dmix", 0),
+                ("mix", 0, 0), ("w", 1, 0), ("dmix", 1), ("wd", 0), ("mix", 0, 1), ("xc", 0, 0), ("xc", 0, 1),
+                ("w", 0, 0), ("x", 0, 0), ("x", 0, 1), ("xc", 0, 2), ("xc", 0, 3), ("w", 0, 1), ("x", 0, 2),
+                ("x", 0, 3), ("dc", 0, 0), ("dc", 0, 1), ("w", 1, 1), ("wd", 1), ("xc", 1, 0), ("xc", 1, 1),
+                ("d", 0, 0), ("d", 0, 1), ("xc", 1, 2), ("xc", 1, 3), ("wide", "S", 0, 1), ("x", 1, 0),
+                ("x", 1, 1), ("dc", 1, 0), ("dc", 1, 1), ("x", 1, 2), ("x", 1, 3), ("wide", "S", 1, 1),
+                ("d", 1, 0), ("d", 1, 1), ("acc",),]
         for c in range(2, BLOCKS):
             prep.append(("dmix", c))
             for g in range(NG):
                 if c % 2 == 0:
-                    prep.append(("wide", g, c // 2))
+                    prep += [("wide", "V", g, c // 2), ("wide", "S", g, c // 2)]
                 prep.append(("mix", g, c))
             if c > 2:
                 prep += [("wd", c - 1), ("w", 0, c - 1), ("w", 1, c - 1)]
@@ -290,16 +320,23 @@ def tile_draft_logit_correction_s7_kernel(tc, x, w_bytes, w_scale, d, w_draft, a
 
         progress = [0, 0]
 
+        def vector_load(key):
+            if key[0] == "wide":
+                return WIDE_ON_VECTOR[key[2]][key[3]] if key[1] == "V" else 0
+            if key[0] == "mix":
+                return 0 if MIX_ON_SCALAR[key[1]][key[2]] else 2
+            if key[0] == "dmix":
+                return 2 if DMIX[key[1]] == "V" else 0
+            if key[0] == "fmix":
+                return 4
+            return 1 if key[0] in ("x", "d", "w", "wd", "f") else 0
+
         def prepare(target):
             while progress[0] < len(prep) and progress[1] < target:
                 key = prep[progress[0]]
                 progress[0] += 1
                 if key not in made:
-                    on_vector = key[0] in ("wide", "fmix", "x", "d", "w", "wd", "f")
-                    if key[0] == "mix":
-                        on_vector = not MIX_ON_SCALAR[key[1]][key[2]]
-                    if on_vector:
-                        progress[1] += WEIGHT.get(key[0], 1)
+                    progress[1] += vector_load(key)
                     need(*key)
 
         n = len(UNITS)

from contextlib import ExitStack

import concourse.mybir as mybir
from concourse.masks import make_identity

T, K, J, V, R = 1024, 1024, 512, 2048, 512
FLOPS = 2 * T * K * V + 2 * T * J * V + 2 * R * T * V

F32 = mybir.dt.float32
BF16 = mybir.dt.bfloat16
U32 = mybir.dt.uint32
U8 = mybir.dt.uint8
FP8 = mybir.dt.float8_e4m3fn
FP8X4 = mybir.dt.float8_e4m3fn_x4
MULT = mybir.AluOpType.mult
ADD = mybir.AluOpType.add
TANH = mybir.ActivationFunctionType.Tanh
COPY = mybir.ActivationFunctionType.Copy

P = 128
NG = 2
NB = 256
BLOCKS = V // NB
SB = 512
RT = R // P
UNITS = [(b, g) for b in range(BLOCKS) for g in range(NG)]
WIDE_ON_VECTOR = [[0, 0, 0, 0], [4, 0, 0, 0]]
MIX_ON_SCALAR = [[0] * 8, [0] * 5 + [1] * 3]
DMIX = "VVVVVVVV"
HEAD, QUOTA, LAG_H, LAG_Q, LAG_C = 53, 3.5, 3, 1, 6


def tile_draft_logit_correction_s7_kernel(tc, x, w_bytes, w_scale, d, w_draft, accept, f, out):
    nc = tc.nc
    with ExitStack() as ctx:
        keep = ctx.enter_context(tc.tile_pool(name="keep", bufs=1))
        work = ctx.enter_context(tc.tile_pool(name="work", bufs=3))
        psum = ctx.enter_context(tc.psum_pool(name="psum", bufs=6))
        opsum = ctx.enter_context(tc.psum_pool(name="opsum", bufs=2))

        ctx.enter_context(tc.manual_schedule())

        x_v = x.rearrange("(g p t) k -> g p t k", p=P, t=4)
        d_v = d.rearrange("(g p t) k -> g p t k", p=P, t=4)
        wb_v = w_bytes.rearrange("(g p t) n -> g p t n", p=P, t=4)
        wd_v = w_draft.rearrange("(p t) n -> p t n", t=4)
        f_v = f.rearrange("(g p t) r -> g p t r", p=P, t=4)
        out_v = out.rearrange("(r p) v -> p r v", p=P)

        raw = {}

        def load(key, shape, dtype, src, queue=nc.sync):
            tile = keep.tile(shape, dtype, name="raw_" + "_".join(str(k) for k in key))
            queue.dma_start(out=tile[:], in_=src)
            raw[key] = tile

        def load_wb(g, s, lo, hi):
            load(("wb", g, s), [P, 4, hi - lo], U8, wb_v[g][:, :, lo:hi])

        def load_wd(s):
            load(("wd", s), [P, 4, SB], BF16, wd_v[:, :, s * SB:(s + 1) * SB])

        def load_x(g, h):
            load(("x", g, h), [P, 2, K], BF16, x_v[g][:, 2 * h:2 * h + 2, :])

        def load_d(g):
            load(("d", g), [P, 4, J], BF16, d_v[g])

        def load_f(g):
            load(("f", g), [P, 4, R], BF16, f_v[g])

        load(("scale",), [P, NG, 4], F32, w_scale.rearrange("(g p t) o -> p g (t o)", p=P, t=4), nc.scalar)
        load_wb(0, 0, 0, 512)
        load_wb(1, 0, 0, 512)
        load_wd(0)
        load_x(0, 0)
        load_x(0, 1)
        load_d(0)
        load_x(1, 0)
        load_x(1, 1)
        load_d(1)
        load_wb(0, 1, 512, 1024)
        load_wb(1, 1, 512, 1024)
        load(("accept",), [P, NG, 4], BF16, accept.rearrange("(g p t) -> p g t", p=P, t=4), nc.scalar)
        load_wd(1)
        load_f(0)
        load_wb(0, 2, 1024, 2048)
        load_wb(1, 2, 1024, 2048)
        load_f(1)
        load_wd(2)
        load_wd(3)
        scale = raw["scale",]

        ident = keep.tile([P, P], F32, name="ident")
        make_identity(nc, ident[:])
        warm = keep.tile([P, 1], F32, name="warm")
        nc.vector.memset(warm[:], 0.0)
        nc.scalar.activation(out=warm[:], in_=warm[:], func=TANH)


        made = {}

        def need(*key):
            if key not in made:
                made[key] = makers[key[0]](*key[1:])
            return made[key]

        def interleaved(dst, src):
            return (dst[:].rearrange("p (c i) t -> p c t i", i=4), src.rearrange("p t (c i) -> p c t i", i=4))

        def quantized(name, src, width):
            codes = keep.tile([P, width], U32, name=name + "_c", align_bytes=64)
            scales = keep.tile([P, width], U8, name=name + "_s", align_bytes=64)
            nc.vector.quantize_mx(out=codes[:].bitcast(FP8X4), scales=scales[:],
                                  in_=src[:].rearrange("p n j -> p (n j)"))
            return codes, scales

        def turn(g, views):
            bank = psum.tile([P, 2, 2, P], F32, name="turned", tag="bank")
            for i, words in enumerate(views):
                for u in range(2):
                    nc.tensor.transpose(bank[:, i, u, :], words[:, u::2], ident[:])
            return bank

        def make_xt(g, t):
            words = raw["x", g, t // 2][:, t % 2, :].bitcast(F32)
            return turn(g, [words[:, 0:256], words[:, 256:512]])

        def make_dt(g, h):
            return turn(g, [raw["d", g][:, 2 * h + i, :].bitcast(F32) for i in range(2)])

        def emptied(bank):
            tok = work.tile([P, 2 * P, 4], BF16, name="tok", tag="tok", bufs=6, align_bytes=64)
            nc.scalar.copy(out=tok[:].bitcast(F32).rearrange("p (i r) u -> p i r u", i=2),
                           in_=bank[:].rearrange("p i u r -> p i r u"))
            return tok

        def make_xc(g, t):
            return emptied(need("xt", g, t))

        def make_dc(g, h):
            return emptied(need("dt", g, h))

        def make_x(g, t):
            return quantized("x_%d_%d" % (g, t), need("xc", g, t), 2 * P)

        def make_d(g, h):
            return quantized("d_%d_%d" % (g, h), need("dc", g, h), 2 * P)

        def make_plain(g, s):
            return work.tile([P, 4, SB], BF16, name="plain", tag="plain", bufs=5)

        def make_wide(engine, g, s):
            plain = need("plain", g, s)
            src = raw["wb", g, min(s, 2)]
            lo = 0 if s < 3 else SB
            cut = WIDE_ON_VECTOR[g][s]
            for t in (range(cut) if engine == "V" else range(cut, 4)):
                codes = src[:, t, lo:lo + SB].bitcast(FP8)
                if engine == "V":
                    nc.vector.tensor_scalar(out=plain[:, t, :], in0=codes, scalar1=scale[:, g, t:t + 1], scalar2=None, op0=MULT)
                else:
                    nc.scalar.activation(out=plain[:, t, :], in_=codes, func=COPY, scale=scale[:, g, t:t + 1])
            return plain

        def make_mix(g, c):
            lo = c % 2 * NB
            need("wide", "V", g, c // 2)
            src = need("wide", "S", g, c // 2)[:, :, lo:lo + NB]
            mixed = work.tile([P, NB, 4], BF16, name="mixed", tag="mixed", bufs=10, align_bytes=64)
            o, i = interleaved(mixed, src)
            if MIX_ON_SCALAR[g][c]:
                nc.scalar.copy(out=o, in_=i)
            else:
                nc.vector.tensor_copy(out=o, in_=i)
            return mixed

        def make_dmix(c):
            lo = c % 2 * NB
            src = raw["wd", c // 2][:, :, lo:lo + NB]
            if DMIX[c] == "G":
                dmixed = work.tile([P, NB, 4], BF16, name="gmixed", tag="gmixed", bufs=2, align_bytes=64)
                o, i = interleaved(dmixed, src)
                for h in range(2):
                    nc.gpsimd.tensor_scalar(out=o[:, 32 * h:32 * h + 32], in0=i[:, 32 * h:32 * h + 32], scalar1=-1.0, scalar2=0.0, op0=MULT, op1=ADD)
                return dmixed
            dmixed = work.tile([P, NB, 4], BF16, name="dmixed", tag="mixed", bufs=10, align_bytes=64)
            o, i = interleaved(dmixed, src)
            if DMIX[c] == "S":
                nc.scalar.activation(out=o, in_=i, func=COPY, scale=-1.0)
            else:
                nc.vector.tensor_scalar(out=o, in0=i, scalar1=-1.0, scalar2=None, op0=MULT)
            return dmixed

        def make_w(g, c):
            return quantized("w_%d_%d" % (g, c), need("mix", g, c), NB)

        def make_wd(c):
            return quantized("wd_%d" % c, need("dmix", c), NB)

        def make_fmix(g):
            fmixed = keep.tile([P, R, 4], BF16, name="fmixed_%d" % g, align_bytes=64)
            o, i = interleaved(fmixed, raw["f", g][:])
            nc.vector.tensor_copy(out=o, in_=i)
            return fmixed

        def make_f(g):
            return quantized("f_%d" % g, need("fmix", g), R)

        def make_acc():
            acc = keep.tile([P, NG, 4], F32, name="acc")
            nc.vector.tensor_copy(out=acc[:], in_=raw["accept",][:])
            return acc

        def make_tanh(b, g):
            th = work.tile([P, 2, NB, 2], F32, name="th", tag="th", bufs=6)
            terms = [(lambda t: [v[:, 0:P] for v in need("x", g, t)], need("w", 0, b)),
                     (lambda t: [v[:, P:2 * P] for v in need("x", g, t)], need("w", 1, b)),
                     (lambda t: [v[:, t % 2 * P:t % 2 * P + P] for v in need("d", g, t // 2)], need("wd", b))]
            for t in range(4):
                need("x", g, t)
            need("d", g, 0)
            need("d", g, 1)
            for h in range(2):
                bank = psum.tile([P, 2, NB], F32, name="logits", tag="bank")
                for jj in range(2):
                    for k, (left, right) in enumerate(terms):
                        lc, ls = left(2 * h + jj)
                        nc.tensor.matmul_mx(out=bank[:, jj, :], lhsT=lc.bitcast(FP8X4), lhsT_scale=ls,
                                            rhs=right[0][:].bitcast(FP8X4), rhs_scale=right[1][:],
                                            start=(k == 0), stop=(k == 2))
                nc.scalar.activation(out=th[:, h, :, :], in_=bank[:].rearrange("p j n -> p n j"), func=TANH)
            return th

        def make_slope(b, g):
            th = need("tanh", b, g)
            e = work.tile([P, NB, 4], BF16, name="e", tag="e", bufs=4, align_bytes=64)
            a = need("acc")[:, g, :].rearrange("p (h j) -> p h j", j=2).unsqueeze(1).to_broadcast([P, NB, 2, 2])
            nc.vector.tensor_tensor(out=e[:].rearrange("p n (h j) -> p n h j", j=2),
                                    in0=th[:].rearrange("p h n j -> p n h j"), in1=a, op=MULT)
            return e

        def make_e(b, g):
            e = need("slope", b, g)
            codes = work.tile([P, NB], U32, name="ec", tag="ec", bufs=12, align_bytes=64)
            scales = work.tile([P, NB], U8, name="es", tag="es", bufs=12, align_bytes=64)
            nc.vector.quantize_mx(out=codes[:].bitcast(FP8X4), scales=scales[:],
                                  in_=e[:].rearrange("p n j -> p (n j)"))
            return codes, scales

        def make_last(b):
            banks = []
            for g in range(NG):
                fc, fs = need("f", g)
                ec, es = need("e", b, g)
                for r in range(RT):
                    if g == 0:
                        last = psum.tile([P, NB], F32, name="last", tag="bank")
                        banks.append(last)
                    nc.tensor.matmul_mx(out=banks[r][:], lhsT=fc[:, r * P:(r + 1) * P].bitcast(FP8X4),
                                        lhsT_scale=fs[:, r * P:(r + 1) * P],
                                        rhs=ec[:].bitcast(FP8X4), rhs_scale=es[:],
                                        start=(g == 0), stop=(g == 1))
            for r in range(RT):
                res = work.tile([P, NB], F32, name="res", tag="res", bufs=6)
                if r % 2 == 0:
                    nc.vector.tensor_copy(out=res[:], in_=banks[r][:])
                else:
                    nc.scalar.copy(out=res[:], in_=banks[r][:])
                nc.sync.dma_start(out=out_v[:, r, b * NB:(b + 1) * NB], in_=res[:])
            return True

        def make_out(b):
            if b == BLOCKS - 1:
                return make_last(b)
            for g in range(NG):
                need("e", b, g)
                need("f", g)
            for q in range(2):
                res = work.tile([P, 2, NB], F32, name="res", tag="res", bufs=6)
                bank = opsum.tile([P, 2, NB], F32, name="sums", tag="sums")
                for jj in range(2):
                    r = 2 * q + jj
                    for g in range(NG):
                        fc, fs = need("f", g)
                        ec, es = need("e", b, g)
                        nc.tensor.matmul_mx(out=bank[:, jj, :], lhsT=fc[:, r * P:(r + 1) * P].bitcast(FP8X4),
                                            lhsT_scale=fs[:, r * P:(r + 1) * P],
                                            rhs=ec[:].bitcast(FP8X4), rhs_scale=es[:],
                                            start=(g == 0), stop=(g == 1))
                nc.scalar.copy(out=res[:], in_=bank[:])
                nc.sync.dma_start(out=out_v[:, 2 * q:2 * q + 2, b * NB:(b + 1) * NB], in_=res[:])
            return True

        makers = {"xt": make_xt, "dt": make_dt, "xc": make_xc, "dc": make_dc, "x": make_x, "d": make_d,
                  "plain": make_plain, "wide": make_wide, "mix": make_mix, "dmix": make_dmix, "w": make_w, "wd": make_wd,
                  "fmix": make_fmix, "f": make_f, "acc": make_acc, "tanh": make_tanh, "slope": make_slope,
                  "e": make_e, "out": make_out}

        prep = [("wide", "S", 0, 0), ("wide", "V", 1, 0), ("mix", 1, 0), ("mix", 1, 1), ("dmix", 0),
                ("mix", 0, 0), ("w", 1, 0), ("dmix", 1), ("wd", 0), ("mix", 0, 1), ("xc", 0, 0), ("xc", 0, 1),
                ("w", 0, 0), ("x", 0, 0), ("x", 0, 1), ("xc", 0, 2), ("xc", 0, 3), ("w", 0, 1), ("x", 0, 2),
                ("x", 0, 3), ("dc", 0, 0), ("dc", 0, 1), ("w", 1, 1), ("wd", 1), ("xc", 1, 0), ("xc", 1, 1),
                ("d", 0, 0), ("d", 0, 1), ("xc", 1, 2), ("xc", 1, 3), ("wide", "S", 0, 1), ("x", 1, 0),
                ("x", 1, 1), ("dc", 1, 0), ("dc", 1, 1), ("x", 1, 2), ("x", 1, 3), ("wide", "S", 1, 1),
                ("d", 1, 0), ("d", 1, 1), ("acc",),]
        for c in range(2, BLOCKS):
            prep.append(("dmix", c))
            for g in range(NG):
                if c % 2 == 0:
                    prep += [("wide", "V", g, c // 2), ("wide", "S", g, c // 2)]
                prep.append(("mix", g, c))
            if c > 2:
                prep += [("wd", c - 1), ("w", 0, c - 1), ("w", 1, c - 1)]
            if c < 4:
                prep.append(("fmix", c - 2))
            if c in (3, 5):
                prep.append(("f", c // 2 - 1))
        prep += [("wd", BLOCKS - 1), ("w", 0, BLOCKS - 1), ("w", 1, BLOCKS - 1)]

        progress = [0, 0]

        def vector_load(key):
            if key[0] == "wide":
                return WIDE_ON_VECTOR[key[2]][key[3]] if key[1] == "V" else 0
            if key[0] == "mix":
                return 0 if MIX_ON_SCALAR[key[1]][key[2]] else 2
            if key[0] == "dmix":
                return 2 if DMIX[key[1]] == "V" else 0
            if key[0] == "fmix":
                return 4
            return 1 if key[0] in ("x", "d", "w", "wd", "f") else 0

        def prepare(target):
            while progress[0] < len(prep) and progress[1] < target:
                key = prep[progress[0]]
                progress[0] += 1
                if key not in made:
                    progress[1] += vector_load(key)
                    need(*key)

        n = len(UNITS)
        prepare(HEAD)
        for i in range(n + LAG_C + 2):
            if i < n:
                need("tanh", *UNITS[i])
            prepare(HEAD + QUOTA * (i + 1))
            if 0 <= i - LAG_H < n:
                need("slope", *UNITS[i - LAG_H])
            if 0 <= i - LAG_H - LAG_Q < n:
                need("e", *UNITS[i - LAG_H - LAG_Q])

            if 0 <= i - LAG_C < n and UNITS[i - LAG_C][1] == 1:
                need("out", UNITS[i - LAG_C][0])
